import numpy as np
CORES = [40,168,296,424]
N = 4
def setup_inputs(rng):
    return {"x": rng.standard_normal((N, 128, 256), dtype=np.float32)}
def reference(x):
    g = np.concatenate(list(x), axis=1)
    return {"y": np.broadcast_to(g, (N,) + g.shape)}

@@ -1,0 +1,32 @@
+W = 256
+
+SCRATCH = {
+    "land": ("sbuf", [128, 4 * W], "float32"),
+}
+SEMAPHORES = ["loaded", "sent", "from_left", "from_right", "from_diag", "stored"]
+
+
+def rank_program(g, core, T, topo):
+    r = T.rank_of(core)
+    if r is None:
+        return
+    nxt, prv = T.cores[(r + 1) % 4], T.cores[(r - 1) % 4]
+
+    def blk(j):
+        return T.land[:, W * j:W * (j + 1)]
+
+    def send(j, dst, sem):
+        rid, pid = topo.addr(dst, core)
+        g.remote_dma(blk(j), blk(j), sem, T.sem.sent, pid, rid, topo.mask(core, dst))
+
+    g.dma_start(blk(r), T.x[:, :]).then_inc(T.sem.loaded, 16)
+    g.wait_ge(T.sem.loaded, 16)
+    send(r, nxt, T.sem.from_left)
+    send(r, prv, T.sem.from_right)
+    g.wait_ge(T.sem.from_left, 8)
+    send((r - 1) % 4, nxt, T.sem.from_diag)
+    g.wait_ge(T.sem.from_right, 8)
+    g.wait_ge(T.sem.from_diag, 8)
+    g.wait_ge(T.sem.sent, 24)
+    g.dma_start(T.y[:, :], T.land[:, :]).then_inc(T.sem.stored, 16)
+    g.wait_ge(T.sem.stored, 16)

@@ -1,32 +1,49 @@
+from concourse.bass import DstId, RemoteDMATransfer
+
 W = 256
+H = W // 2
 
 SCRATCH = {
     "land": ("sbuf", [128, 4 * W], "float32"),
 }
-SEMAPHORES = ["loaded", "sent", "from_left", "from_right", "from_diag", "stored"]
+SEMAPHORES = ["loaded", "sent", "l_first", "l_rest", "r_first", "r_rest", "diag", "stored"]
+
+TO_NXT, TO_PRV = 0x0F, 0xF0
 
 
 def rank_program(g, core, T, topo):
     r = T.rank_of(core)
     if r is None:
         return
-    nxt, prv = T.cores[(r + 1) % 4], T.cores[(r - 1) % 4]
+    S = T.sem
+    left, right = (r - 1) % 4, (r + 1) % 4
+    nxt, prv = T.cores[right], T.cores[left]
+
+    def half(j, h):
+        return T.land[:, W * j + H * h:W * j + H * (h + 1)]
 
     def blk(j):
         return T.land[:, W * j:W * (j + 1)]
 
-    def send(j, dst, sem):
+    def tr(j, h, dst, mask, sem):
         rid, pid = topo.addr(dst, core)
-        g.remote_dma(blk(j), blk(j), sem, T.sem.sent, pid, rid, topo.mask(core, dst))
+        return RemoteDMATransfer(dst_ids=[DstId(rid=rid, pnc=pid)], dma_engine_mask=mask, remote_sem=sem,
+                                 src=half(j, h), dst=half(j, h))
 
-    g.dma_start(blk(r), T.x[:, :]).then_inc(T.sem.loaded, 16)
-    g.wait_ge(T.sem.loaded, 16)
-    send(r, nxt, T.sem.from_left)
-    send(r, prv, T.sem.from_right)
-    g.wait_ge(T.sem.from_left, 8)
-    send((r - 1) % 4, nxt, T.sem.from_diag)
-    g.wait_ge(T.sem.from_right, 8)
-    g.wait_ge(T.sem.from_diag, 8)
-    g.wait_ge(T.sem.sent, 24)
-    g.dma_start(T.y[:, :], T.land[:, :]).then_inc(T.sem.stored, 16)
-    g.wait_ge(T.sem.stored, 16)
+    g.dma_start(blk(r), T.x[:, :]).then_inc(S.loaded, 16)
+    g.wait_ge(S.loaded, 16)
+    g.remote_dma_fused([tr(r, 0, nxt, TO_NXT, S.l_first), tr(r, 1, prv, TO_PRV, S.r_first)], local_sem=S.sent)
+    g.remote_dma_fused([tr(r, 1, nxt, TO_NXT, S.l_rest), tr(r, 0, prv, TO_PRV, S.r_rest)], local_sem=S.sent)
+    g.dma_start(T.y[:, W * r:W * (r + 1)], T.x[:, :]).then_inc(S.stored, 16)
+    g.wait_ge(S.l_first, 4)
+    g.wait_ge(S.r_first, 4)
+    g.remote_dma_fused([tr(left, 0, nxt, TO_NXT, S.diag), tr(right, 1, prv, TO_PRV, S.diag)], local_sem=S.sent)
+    g.wait_ge(S.l_rest, 4)
+    g.dma_start(T.y[:, W * left:W * (left + 1)], blk(left)).then_inc(S.stored, 16)
+    g.wait_ge(S.r_rest, 4)
+    g.dma_start(T.y[:, W * right:W * (right + 1)], blk(right)).then_inc(S.stored, 16)
+    d = (r + 2) % 4
+    g.wait_ge(S.diag, 8)
+    g.dma_start(T.y[:, W * d:W * (d + 1)], blk(d)).then_inc(S.stored, 16)
+    g.wait_ge(S.sent, 24)
+    g.wait_ge(S.stored, 64)

@@ -6,18 +6,20 @@ H = W // 2
 SCRATCH = {
     "land": ("sbuf", [128, 4 * W], "float32"),
 }
-SEMAPHORES = ["loaded", "sent", "l_first", "l_rest", "r_first", "r_rest", "diag", "stored"]
+SEMAPHORES = ["loaded", "sent", "relay", "l_first", "l_rest", "r_first", "r_rest", "diag", "stored"]
 
 TO_NXT, TO_PRV = 0x0F, 0xF0
+OFF_CHIP, ON_CHIP = 0x00FF, 0xFF00
+SWITCH_HELPER, CABLE_HELPER = 4, 2
+
+
+def helper(T, q, up):
+    by_switch = (q % 2 == 0) == up
+    return T.cores[q] + (SWITCH_HELPER if by_switch else CABLE_HELPER)
 
 
 def rank_program(g, core, T, topo):
-    r = T.rank_of(core)
-    if r is None:
-        return
     S = T.sem
-    left, right = (r - 1) % 4, (r + 1) % 4
-    nxt, prv = T.cores[right], T.cores[left]
 
     def half(j, h):
         return T.land[:, W * j + H * h:W * j + H * (h + 1)]
@@ -30,20 +32,37 @@ def rank_program(g, core, T, topo):
         return RemoteDMATransfer(dst_ids=[DstId(rid=rid, pnc=pid)], dma_engine_mask=mask, remote_sem=sem,
                                  src=half(j, h), dst=half(j, h))
 
+    r = T.rank_of(core)
+    if r is None:
+        q = T.rank_of(core - core % 8)
+        if q is None:
+            return
+        for up in (True, False):
+            if core == helper(T, q, up):
+                j, h = ((q - 1) % 4, 0) if up else ((q + 1) % 4, 1)
+                far = T.cores[(q + 1) % 4] if up else T.cores[(q - 1) % 4]
+                g.wait_ge(S.relay, 4)
+                g.remote_dma_fused([tr(j, h, far, OFF_CHIP, S.diag),
+                                    tr(j, h, T.cores[q], ON_CHIP, S.l_first if up else S.r_first)], local_sem=S.sent)
+                g.wait_ge(S.sent, 16)
+        return
+
+    left, right, d = (r - 1) % 4, (r + 1) % 4, (r + 2) % 4
+    nxt, prv = T.cores[right], T.cores[left]
+
     g.dma_start(blk(r), T.x[:, :]).then_inc(S.loaded, 16)
     g.wait_ge(S.loaded, 16)
-    g.remote_dma_fused([tr(r, 0, nxt, TO_NXT, S.l_first), tr(r, 1, prv, TO_PRV, S.r_first)], local_sem=S.sent)
+    g.remote_dma_fused([tr(r, 0, helper(T, right, True), TO_NXT, S.relay),
+                        tr(r, 1, helper(T, left, False), TO_PRV, S.relay)], local_sem=S.sent)
     g.remote_dma_fused([tr(r, 1, nxt, TO_NXT, S.l_rest), tr(r, 0, prv, TO_PRV, S.r_rest)], local_sem=S.sent)
     g.dma_start(T.y[:, W * r:W * (r + 1)], T.x[:, :]).then_inc(S.stored, 16)
-    g.wait_ge(S.l_first, 4)
-    g.wait_ge(S.r_first, 4)
-    g.remote_dma_fused([tr(left, 0, nxt, TO_NXT, S.diag), tr(right, 1, prv, TO_PRV, S.diag)], local_sem=S.sent)
     g.wait_ge(S.l_rest, 4)
+    g.wait_ge(S.l_first, 8)
     g.dma_start(T.y[:, W * left:W * (left + 1)], blk(left)).then_inc(S.stored, 16)
     g.wait_ge(S.r_rest, 4)
+    g.wait_ge(S.r_first, 8)
     g.dma_start(T.y[:, W * right:W * (right + 1)], blk(right)).then_inc(S.stored, 16)
-    d = (r + 2) % 4
-    g.wait_ge(S.diag, 8)
+    g.wait_ge(S.diag, 16)
     g.dma_start(T.y[:, W * d:W * (d + 1)], blk(d)).then_inc(S.stored, 16)
-    g.wait_ge(S.sent, 24)
+    g.wait_ge(S.sent, 16)
     g.wait_ge(S.stored, 64)

@@ -1,36 +1,35 @@
 from concourse.bass import DstId, RemoteDMATransfer
 
 W = 256
-H = W // 2
+K = 2
+C = K // 2
+R = 128 // K
 
 SCRATCH = {
-    "land": ("sbuf", [128, 4 * W], "float32"),
+    "land": ("dram", [4 * K, 128, W // K], "float32"),
 }
 SEMAPHORES = ["loaded", "sent", "relay", "l_first", "l_rest", "r_first", "r_rest", "diag", "stored"]
 
 TO_NXT, TO_PRV = 0x0F, 0xF0
 OFF_CHIP, ON_CHIP = 0x00FF, 0xFF00
-SWITCH_HELPER, CABLE_HELPER = 4, 2
+SWITCH_HELPERS, CABLE_HELPERS = (4, 5), (2, 6)
 
 
-def helper(T, q, up):
+def helper(T, q, up, i):
     by_switch = (q % 2 == 0) == up
-    return T.cores[q] + (SWITCH_HELPER if by_switch else CABLE_HELPER)
+    return T.cores[q] + (SWITCH_HELPERS if by_switch else CABLE_HELPERS)[i]
 
 
 def rank_program(g, core, T, topo):
     S = T.sem
 
-    def half(j, h):
-        return T.land[:, W * j + H * h:W * j + H * (h + 1)]
-
-    def blk(j):
-        return T.land[:, W * j:W * (j + 1)]
-
-    def tr(j, h, dst, mask, sem):
+    def tr(j, c, dst, mask, sem):
         rid, pid = topo.addr(dst, core)
         return RemoteDMATransfer(dst_ids=[DstId(rid=rid, pnc=pid)], dma_engine_mask=mask, remote_sem=sem,
-                                 src=half(j, h), dst=half(j, h))
+                                 src=T.land[K * j + c], dst=T.land[K * j + c])
+
+    def store(j):
+        g.dma_start(T.y[:, W * j:W * (j + 1)], T.land[K * j:K * (j + 1)]).then_inc(S.stored, 16)
 
     r = T.rank_of(core)
     if r is None:
@@ -38,31 +37,35 @@ def rank_program(g, core, T, topo):
         if q is None:
             return
         for up in (True, False):
-            if core == helper(T, q, up):
-                j, h = ((q - 1) % 4, 0) if up else ((q + 1) % 4, 1)
-                far = T.cores[(q + 1) % 4] if up else T.cores[(q - 1) % 4]
-                g.wait_ge(S.relay, 4)
-                g.remote_dma_fused([tr(j, h, far, OFF_CHIP, S.diag),
-                                    tr(j, h, T.cores[q], ON_CHIP, S.l_first if up else S.r_first)], local_sem=S.sent)
-                g.wait_ge(S.sent, 16)
+            for i in range(C):
+                if core == helper(T, q, up, i):
+                    j, c = ((q - 1) % 4, i) if up else ((q + 1) % 4, C + i)
+                    far = T.cores[(q + 1) % 4] if up else T.cores[(q - 1) % 4]
+                    g.wait_ge(S.relay, 4)
+                    g.remote_dma_fused([tr(j, c, far, OFF_CHIP, S.diag),
+                                        tr(j, c, T.cores[q], ON_CHIP, S.l_first if up else S.r_first)],
+                                       local_sem=S.sent)
+                    g.wait_ge(S.sent, 16)
         return
 
     left, right, d = (r - 1) % 4, (r + 1) % 4, (r + 2) % 4
     nxt, prv = T.cores[right], T.cores[left]
 
-    g.dma_start(blk(r), T.x[:, :]).then_inc(S.loaded, 16)
+    g.dma_start(T.land[K * r:K * (r + 1)], T.x[:, :]).then_inc(S.loaded, 16)
     g.wait_ge(S.loaded, 16)
-    g.remote_dma_fused([tr(r, 0, helper(T, right, True), TO_NXT, S.relay),
-                        tr(r, 1, helper(T, left, False), TO_PRV, S.relay)], local_sem=S.sent)
-    g.remote_dma_fused([tr(r, 1, nxt, TO_NXT, S.l_rest), tr(r, 0, prv, TO_PRV, S.r_rest)], local_sem=S.sent)
+    for i in range(C):
+        g.remote_dma_fused([tr(r, i, helper(T, right, True, i), TO_NXT, S.relay),
+                            tr(r, C + i, helper(T, left, False, i), TO_PRV, S.relay)], local_sem=S.sent)
+    for i in range(C):
+        g.remote_dma_fused([tr(r, C + i, nxt, TO_NXT, S.l_rest), tr(r, i, prv, TO_PRV, S.r_rest)], local_sem=S.sent)
     g.dma_start(T.y[:, W * r:W * (r + 1)], T.x[:, :]).then_inc(S.stored, 16)
-    g.wait_ge(S.l_rest, 4)
-    g.wait_ge(S.l_first, 8)
-    g.dma_start(T.y[:, W * left:W * (left + 1)], blk(left)).then_inc(S.stored, 16)
-    g.wait_ge(S.r_rest, 4)
-    g.wait_ge(S.r_first, 8)
-    g.dma_start(T.y[:, W * right:W * (right + 1)], blk(right)).then_inc(S.stored, 16)
-    g.wait_ge(S.diag, 16)
-    g.dma_start(T.y[:, W * d:W * (d + 1)], blk(d)).then_inc(S.stored, 16)
-    g.wait_ge(S.sent, 16)
+    g.wait_ge(S.l_rest, 4 * C)
+    g.wait_ge(S.l_first, 8 * C)
+    store(left)
+    g.wait_ge(S.r_rest, 4 * C)
+    g.wait_ge(S.r_first, 8 * C)
+    store(right)
+    g.wait_ge(S.diag, 16 * C)
+    store(d)
+    g.wait_ge(S.sent, 16 * C)
     g.wait_ge(S.stored, 64)

@@ -1,14 +1,15 @@
 from concourse.bass import DstId, RemoteDMATransfer
 
 W = 256
-K = 2
+K = 4
 C = K // 2
 R = 128 // K
 
 SCRATCH = {
     "land": ("dram", [4 * K, 128, W // K], "float32"),
 }
-SEMAPHORES = ["loaded", "sent", "relay", "l_first", "l_rest", "r_first", "r_rest", "diag", "stored"]
+SEMAPHORES = (["sent", "relay", "l_first", "l_rest", "r_first", "r_rest", "stored"]
+              + ["loaded%d" % i for i in range(C)] + ["diag%d" % i for i in range(C)])
 
 TO_NXT, TO_PRV = 0x0F, 0xF0
 OFF_CHIP, ON_CHIP = 0x00FF, 0xFF00
@@ -22,14 +23,13 @@ def helper(T, q, up, i):
 
 def rank_program(g, core, T, topo):
     S = T.sem
+    loaded = [S.loaded0, S.loaded1]
+    diag = [S.diag0, S.diag1]
 
     def tr(j, c, dst, mask, sem):
         rid, pid = topo.addr(dst, core)
         return RemoteDMATransfer(dst_ids=[DstId(rid=rid, pnc=pid)], dma_engine_mask=mask, remote_sem=sem,
                                  src=T.land[K * j + c], dst=T.land[K * j + c])
-
-    def store(j):
-        g.dma_start(T.y[:, W * j:W * (j + 1)], T.land[K * j:K * (j + 1)]).then_inc(S.stored, 16)
 
     r = T.rank_of(core)
     if r is None:
@@ -39,10 +39,10 @@ def rank_program(g, core, T, topo):
         for up in (True, False):
             for i in range(C):
                 if core == helper(T, q, up, i):
-                    j, c = ((q - 1) % 4, i) if up else ((q + 1) % 4, C + i)
+                    j, c = ((q - 1) % 4, 2 * i) if up else ((q + 1) % 4, 2 * i + 1)
                     far = T.cores[(q + 1) % 4] if up else T.cores[(q - 1) % 4]
                     g.wait_ge(S.relay, 4)
-                    g.remote_dma_fused([tr(j, c, far, OFF_CHIP, S.diag),
+                    g.remote_dma_fused([tr(j, c, far, OFF_CHIP, diag[i]),
                                         tr(j, c, T.cores[q], ON_CHIP, S.l_first if up else S.r_first)],
                                        local_sem=S.sent)
                     g.wait_ge(S.sent, 16)
@@ -51,21 +51,31 @@ def rank_program(g, core, T, topo):
     left, right, d = (r - 1) % 4, (r + 1) % 4, (r + 2) % 4
     nxt, prv = T.cores[right], T.cores[left]
 
-    g.dma_start(T.land[K * r:K * (r + 1)], T.x[:, :]).then_inc(S.loaded, 16)
-    g.wait_ge(S.loaded, 16)
+    def store_block(j):
+        g.dma_start(T.y[:, W * j:W * (j + 1)], T.land[K * j:K * (j + 1)]).then_inc(S.stored, 16)
+
+    def store_diag(i):
+        g.wait_ge(diag[i], 16)
+        g.dma_start(T.y[2 * i * R:(2 * i + 2) * R, W * d:W * (d + 1)],
+                    T.land[K * d + 2 * i:K * d + 2 * i + 2]).then_inc(S.stored, 16)
+
     for i in range(C):
-        g.remote_dma_fused([tr(r, i, helper(T, right, True, i), TO_NXT, S.relay),
-                            tr(r, C + i, helper(T, left, False, i), TO_PRV, S.relay)], local_sem=S.sent)
+        g.dma_start(T.land[K * r + 2 * i:K * r + 2 * i + 2], T.x[2 * i * R:(2 * i + 2) * R, :]).then_inc(loaded[i], 16)
     for i in range(C):
-        g.remote_dma_fused([tr(r, C + i, nxt, TO_NXT, S.l_rest), tr(r, i, prv, TO_PRV, S.r_rest)], local_sem=S.sent)
+        g.wait_ge(loaded[i], 16)
+        g.remote_dma_fused([tr(r, 2 * i, helper(T, right, True, i), TO_NXT, S.relay),
+                            tr(r, 2 * i + 1, helper(T, left, False, i), TO_PRV, S.relay)], local_sem=S.sent)
+    g.remote_dma_fused([tr(r, 2 * i + 1, nxt, 0x03 << (2 * i), S.l_rest) for i in range(C)]
+                       + [tr(r, 2 * i, prv, 0x30 << (2 * i), S.r_rest) for i in range(C)], local_sem=S.sent)
     g.dma_start(T.y[:, W * r:W * (r + 1)], T.x[:, :]).then_inc(S.stored, 16)
-    g.wait_ge(S.l_rest, 4 * C)
+    for i in range(C - 1):
+        store_diag(i)
+    g.wait_ge(S.l_rest, 2 * C)
     g.wait_ge(S.l_first, 8 * C)
-    store(left)
-    g.wait_ge(S.r_rest, 4 * C)
+    store_block(left)
+    g.wait_ge(S.r_rest, 2 * C)
     g.wait_ge(S.r_first, 8 * C)
-    store(right)
-    g.wait_ge(S.diag, 16 * C)
-    store(d)
-    g.wait_ge(S.sent, 16 * C)
-    g.wait_ge(S.stored, 64)
+    store_block(right)
+    store_diag(C - 1)
+    g.wait_ge(S.sent, 8 * C + 8)
+    g.wait_ge(S.stored, 48 + 16 * C)

@@ -2,23 +2,32 @@ from concourse.bass import DstId, RemoteDMATransfer
 
 W = 256
 K = 4
-C = K // 2
+C = 2
 R = 128 // K
 
 SCRATCH = {
     "land": ("dram", [4 * K, 128, W // K], "float32"),
 }
-SEMAPHORES = (["sent", "relay", "l_first", "l_rest", "r_first", "r_rest", "stored"]
-              + ["loaded%d" % i for i in range(C)] + ["diag%d" % i for i in range(C)])
+SEMAPHORES = ["sent", "relay", "spread", "l_first", "l_rest", "r_first", "r_rest", "stored",
+              "loaded0", "loaded1", "diag0", "diag1"]
 
-TO_NXT, TO_PRV = 0x0F, 0xF0
 OFF_CHIP, ON_CHIP = 0x00FF, 0xFF00
-SWITCH_HELPERS, CABLE_HELPERS = (4, 5), (2, 6)
+TO_NXT, TO_PRV = 0x000F, 0x00F0
+SPREAD_NXT, SPREAD_PRV = 0x0F00, 0xF000
+SWITCH_RELAYS, SWITCH_SPREADER = (6, 7), 5
+CABLE_RELAYS, CABLE_SPREADER = (2, 3), 4
 
 
-def helper(T, q, up, i):
-    by_switch = (q % 2 == 0) == up
-    return T.cores[q] + (SWITCH_HELPERS if by_switch else CABLE_HELPERS)[i]
+def by_switch(q, up):
+    return (q % 2 == 0) == up
+
+
+def relay(T, q, up, i):
+    return T.cores[q] + (SWITCH_RELAYS if by_switch(q, up) else CABLE_RELAYS)[i]
+
+
+def spreader(T, q, up):
+    return T.cores[q] + (SWITCH_SPREADER if by_switch(q, up) else CABLE_SPREADER)
 
 
 def rank_program(g, core, T, topo):
@@ -37,15 +46,20 @@ def rank_program(g, core, T, topo):
         if q is None:
             return
         for up in (True, False):
+            far = T.cores[(q + 1) % 4] if up else T.cores[(q - 1) % 4]
             for i in range(C):
-                if core == helper(T, q, up, i):
+                if core == relay(T, q, up, i):
                     j, c = ((q - 1) % 4, 2 * i) if up else ((q + 1) % 4, 2 * i + 1)
-                    far = T.cores[(q + 1) % 4] if up else T.cores[(q - 1) % 4]
                     g.wait_ge(S.relay, 4)
                     g.remote_dma_fused([tr(j, c, far, OFF_CHIP, diag[i]),
                                         tr(j, c, T.cores[q], ON_CHIP, S.l_first if up else S.r_first)],
                                        local_sem=S.sent)
                     g.wait_ge(S.sent, 16)
+            if core == spreader(T, q, up):
+                g.wait_ge(S.spread, 4)
+                g.remote_dma_fused([tr(q, 1 if up else 0, far, OFF_CHIP, S.l_rest if up else S.r_rest)],
+                                   local_sem=S.sent)
+                g.wait_ge(S.sent, 8)
         return
 
     left, right, d = (r - 1) % 4, (r + 1) % 4, (r + 2) % 4
@@ -61,21 +75,23 @@ def rank_program(g, core, T, topo):
 
     for i in range(C):
         g.dma_start(T.land[K * r + 2 * i:K * r + 2 * i + 2], T.x[2 * i * R:(2 * i + 2) * R, :]).then_inc(loaded[i], 16)
-    for i in range(C):
-        g.wait_ge(loaded[i], 16)
-        g.remote_dma_fused([tr(r, 2 * i, helper(T, right, True, i), TO_NXT, S.relay),
-                            tr(r, 2 * i + 1, helper(T, left, False, i), TO_PRV, S.relay)], local_sem=S.sent)
-    g.remote_dma_fused([tr(r, 2 * i + 1, nxt, 0x03 << (2 * i), S.l_rest) for i in range(C)]
-                       + [tr(r, 2 * i, prv, 0x30 << (2 * i), S.r_rest) for i in range(C)], local_sem=S.sent)
+    g.wait_ge(loaded[0], 16)
+    g.remote_dma_fused([tr(r, 0, relay(T, right, True, 0), TO_NXT, S.relay),
+                        tr(r, 1, relay(T, left, False, 0), TO_PRV, S.relay),
+                        tr(r, 1, spreader(T, r, True), SPREAD_NXT, S.spread),
+                        tr(r, 0, spreader(T, r, False), SPREAD_PRV, S.spread)], local_sem=S.sent)
+    g.wait_ge(loaded[1], 16)
+    g.remote_dma_fused([tr(r, 2, relay(T, right, True, 1), TO_NXT, S.relay),
+                        tr(r, 3, relay(T, left, False, 1), TO_PRV, S.relay)], local_sem=S.sent)
+    g.remote_dma_fused([tr(r, 3, nxt, TO_NXT, S.l_rest), tr(r, 2, prv, TO_PRV, S.r_rest)], local_sem=S.sent)
     g.dma_start(T.y[:, W * r:W * (r + 1)], T.x[:, :]).then_inc(S.stored, 16)
-    for i in range(C - 1):
-        store_diag(i)
-    g.wait_ge(S.l_rest, 2 * C)
-    g.wait_ge(S.l_first, 8 * C)
+    store_diag(0)
+    g.wait_ge(S.l_rest, 12)
+    g.wait_ge(S.l_first, 16)
     store_block(left)
-    g.wait_ge(S.r_rest, 2 * C)
-    g.wait_ge(S.r_first, 8 * C)
+    g.wait_ge(S.r_rest, 12)
+    g.wait_ge(S.r_first, 16)
     store_block(right)
-    store_diag(C - 1)
-    g.wait_ge(S.sent, 8 * C + 8)
-    g.wait_ge(S.stored, 48 + 16 * C)
+    store_diag(1)
+    g.wait_ge(S.sent, 32)
+    g.wait_ge(S.stored, 80)

@@ -1,97 +1,99 @@
 from concourse.bass import DstId, RemoteDMATransfer
 
 W = 256
-K = 4
-C = 2
+K = 8
 R = 128 // K
 
 SCRATCH = {
     "land": ("dram", [4 * K, 128, W // K], "float32"),
 }
-SEMAPHORES = ["sent", "relay", "spread", "l_first", "l_rest", "r_first", "r_rest", "stored",
-              "loaded0", "loaded1", "diag0", "diag1"]
+SEMAPHORES = ["sent", "stored", "loaded_a", "loaded_b", "spread_a", "spread_b", "relay_a", "relay_b",
+              "sw_in", "cb_in", "dg_a", "dg_b"]
 
-OFF_CHIP, ON_CHIP = 0x00FF, 0xFF00
-TO_NXT, TO_PRV = 0x000F, 0x00F0
-SPREAD_NXT, SPREAD_PRV = 0x0F00, 0xF000
-SWITCH_RELAYS, SWITCH_SPREADER = (6, 7), 5
-CABLE_RELAYS, CABLE_SPREADER = (2, 3), 4
-
-
-def by_switch(q, up):
-    return (q % 2 == 0) == up
-
-
-def relay(T, q, up, i):
-    return T.cores[q] + (SWITCH_RELAYS if by_switch(q, up) else CABLE_RELAYS)[i]
-
-
-def spreader(T, q, up):
-    return T.cores[q] + (SWITCH_SPREADER if by_switch(q, up) else CABLE_SPREADER)
+OFF, ON = 0x00FF, 0xFF00
+LO, HI = 0x000F, 0x00F0
+RELAY = {0: (5, 0), 1: (7, 0), 2: (3, 0), 3: (3, 1), 4: (6, 0), 5: (2, 0), 6: (5, 1), 7: (7, 1)}
 
 
 def rank_program(g, core, T, topo):
     S = T.sem
-    loaded = [S.loaded0, S.loaded1]
-    diag = [S.diag0, S.diag1]
+    q = T.rank_of(core - core % 8)
+    if q is None:
+        return
+    me = core % 8
+    sw, cb, dg = q ^ 1, 3 - q, (q + 2) % 4
+    relay_sem = [S.relay_a, S.relay_b]
+    sent = [0]
 
     def tr(j, c, dst, mask, sem):
         rid, pid = topo.addr(dst, core)
+        sent[0] += bin(mask).count("1")
         return RemoteDMATransfer(dst_ids=[DstId(rid=rid, pnc=pid)], dma_engine_mask=mask, remote_sem=sem,
                                  src=T.land[K * j + c], dst=T.land[K * j + c])
 
-    r = T.rank_of(core)
-    if r is None:
-        q = T.rank_of(core - core % 8)
-        if q is None:
-            return
-        for up in (True, False):
-            far = T.cores[(q + 1) % 4] if up else T.cores[(q - 1) % 4]
-            for i in range(C):
-                if core == relay(T, q, up, i):
-                    j, c = ((q - 1) % 4, 2 * i) if up else ((q + 1) % 4, 2 * i + 1)
-                    g.wait_ge(S.relay, 4)
-                    g.remote_dma_fused([tr(j, c, far, OFF_CHIP, diag[i]),
-                                        tr(j, c, T.cores[q], ON_CHIP, S.l_first if up else S.r_first)],
-                                       local_sem=S.sent)
-                    g.wait_ge(S.sent, 16)
-            if core == spreader(T, q, up):
-                g.wait_ge(S.spread, 4)
-                g.remote_dma_fused([tr(q, 1 if up else 0, far, OFF_CHIP, S.l_rest if up else S.r_rest)],
-                                   local_sem=S.sent)
-                g.wait_ge(S.sent, 8)
-        return
+    def to_relay(c, mask):
+        off, which = RELAY[c]
+        return tr(q, c, T.cores[cb if c < 2 else sw] + off, mask, relay_sem[which])
 
-    left, right, d = (r - 1) % 4, (r + 1) % 4, (r + 2) % 4
-    nxt, prv = T.cores[right], T.cores[left]
+    def call(*transfers):
+        g.remote_dma_fused(list(transfers), local_sem=S.sent)
 
-    def store_block(j):
-        g.dma_start(T.y[:, W * j:W * (j + 1)], T.land[K * j:K * (j + 1)]).then_inc(S.stored, 16)
+    def relay(c, n):
+        g.wait_ge(relay_sem[RELAY[c][1]], n)
+        j, far, near_sem = (cb, sw, S.cb_in) if c < 2 else (sw, cb, S.sw_in)
+        call(tr(j, c, T.cores[far], OFF, S.dg_a if c < 4 else S.dg_b), tr(j, c, T.cores[q], ON, near_sem))
 
-    def store_diag(i):
-        g.wait_ge(diag[i], 16)
-        g.dma_start(T.y[2 * i * R:(2 * i + 2) * R, W * d:W * (d + 1)],
-                    T.land[K * d + 2 * i:K * d + 2 * i + 2]).then_inc(S.stored, 16)
+    if me == 0:
+        def rows(a, b):
+            return slice(a * R, b * R)
 
-    for i in range(C):
-        g.dma_start(T.land[K * r + 2 * i:K * r + 2 * i + 2], T.x[2 * i * R:(2 * i + 2) * R, :]).then_inc(loaded[i], 16)
-    g.wait_ge(loaded[0], 16)
-    g.remote_dma_fused([tr(r, 0, relay(T, right, True, 0), TO_NXT, S.relay),
-                        tr(r, 1, relay(T, left, False, 0), TO_PRV, S.relay),
-                        tr(r, 1, spreader(T, r, True), SPREAD_NXT, S.spread),
-                        tr(r, 0, spreader(T, r, False), SPREAD_PRV, S.spread)], local_sem=S.sent)
-    g.wait_ge(loaded[1], 16)
-    g.remote_dma_fused([tr(r, 2, relay(T, right, True, 1), TO_NXT, S.relay),
-                        tr(r, 3, relay(T, left, False, 1), TO_PRV, S.relay)], local_sem=S.sent)
-    g.remote_dma_fused([tr(r, 3, nxt, TO_NXT, S.l_rest), tr(r, 2, prv, TO_PRV, S.r_rest)], local_sem=S.sent)
-    g.dma_start(T.y[:, W * r:W * (r + 1)], T.x[:, :]).then_inc(S.stored, 16)
-    store_diag(0)
-    g.wait_ge(S.l_rest, 12)
-    g.wait_ge(S.l_first, 16)
-    store_block(left)
-    g.wait_ge(S.r_rest, 12)
-    g.wait_ge(S.r_first, 16)
-    store_block(right)
-    store_diag(1)
-    g.wait_ge(S.sent, 32)
-    g.wait_ge(S.stored, 80)
+        def store(j, a, b):
+            g.dma_start(T.y[rows(a, b), W * j:W * (j + 1)], T.land[K * j + a:K * j + b]).then_inc(S.stored, 16)
+
+        g.dma_start(T.land[K * q:K * q + 4], T.x[rows(0, 4), :]).then_inc(S.loaded_a, 16)
+        g.dma_start(T.land[K * q + 4:K * q + 8], T.x[rows(4, 8), :]).then_inc(S.loaded_b, 16)
+        g.wait_ge(S.loaded_a, 16)
+        call(to_relay(2, LO), to_relay(0, HI),
+             tr(q, 3, core + 4, 0x0F00, S.spread_a), tr(q, 1, core + 4, 0xF000, S.spread_b))
+        g.wait_ge(S.loaded_b, 16)
+        call(to_relay(4, LO), to_relay(1, HI),
+             tr(q, 7, core + 4, 0x0F00, S.spread_b), tr(q, 5, core + 2, 0x3000, S.spread_a),
+             tr(q, 6, core + 6, 0xC000, S.spread_a))
+        call(to_relay(5, LO), tr(q, 2, T.cores[cb], HI, S.cb_in))
+        call(to_relay(6, LO), tr(q, 4, T.cores[cb], HI, S.cb_in))
+        call(tr(q, 0, T.cores[sw], LO, S.sw_in), tr(q, 7, T.cores[cb], HI, S.cb_in))
+        g.dma_start(T.y[:, W * q:W * (q + 1)], T.x[:, :]).then_inc(S.stored, 16)
+        g.wait_ge(S.dg_a, 32)
+        store(dg, 0, 4)
+        g.wait_ge(S.cb_in, 48)
+        store(cb, 0, 8)
+        g.wait_ge(S.sw_in, 60)
+        store(sw, 0, 8)
+        g.wait_ge(S.dg_b, 32)
+        store(dg, 4, 8)
+        g.wait_ge(S.stored, 80)
+    elif me == 2:
+        g.wait_ge(S.spread_a, 2)
+        call(tr(q, 5, T.cores[cb], OFF, S.cb_in))
+        relay(5, 4)
+    elif me == 3:
+        relay(2, 4)
+        relay(3, 4)
+    elif me == 4:
+        g.wait_ge(S.spread_a, 4)
+        call(to_relay(3, LO), tr(q, 3, T.cores[cb], HI, S.cb_in))
+        g.wait_ge(S.spread_b, 8)
+        call(to_relay(7, OFF))
+        call(tr(q, 1, T.cores[sw], OFF, S.sw_in))
+    elif me == 5:
+        relay(0, 4)
+        relay(6, 4)
+    elif me == 6:
+        g.wait_ge(S.spread_a, 2)
+        call(tr(q, 6, T.cores[cb], OFF, S.cb_in))
+        relay(4, 4)
+    elif me == 7:
+        relay(1, 4)
+        relay(7, 8)
+    if sent[0]:
+        g.wait_ge(S.sent, sent[0])

from concourse.bass import DstId, RemoteDMATransfer

W = 256
K = 8
R = 128 // K

SCRATCH = {
    "land": ("dram", [4 * K, 128, W // K], "float32"),
}
SEMAPHORES = ["sent", "stored", "loaded_a", "loaded_b", "spread_a", "spread_b", "relay_a", "relay_b",
              "sw_in", "cb_in", "dg_a", "dg_b"]

OFF, ON = 0x00FF, 0xFF00
LO, HI = 0x000F, 0x00F0
RELAY = {0: (5, 0), 1: (7, 0), 2: (3, 0), 3: (3, 1), 4: (6, 0), 5: (2, 0), 6: (5, 1), 7: (7, 1)}


def rank_program(g, core, T, topo):
    S = T.sem
    q = T.rank_of(core - core % 8)
    if q is None:
        return
    me = core % 8
    sw, cb, dg = q ^ 1, 3 - q, (q + 2) % 4
    relay_sem = [S.relay_a, S.relay_b]
    sent = [0]

    def tr(j, c, dst, mask, sem):
        rid, pid = topo.addr(dst, core)
        sent[0] += bin(mask).count("1")
        return RemoteDMATransfer(dst_ids=[DstId(rid=rid, pnc=pid)], dma_engine_mask=mask, remote_sem=sem,
                                 src=T.land[K * j + c], dst=T.land[K * j + c])

    def to_relay(c, mask):
        off, which = RELAY[c]
        return tr(q, c, T.cores[cb if c < 2 else sw] + off, mask, relay_sem[which])

    def call(*transfers):
        g.remote_dma_fused(list(transfers), local_sem=S.sent)

    def relay(c, n):
        g.wait_ge(relay_sem[RELAY[c][1]], n)
        j, far, near_sem = (cb, sw, S.cb_in) if c < 2 else (sw, cb, S.sw_in)
        call(tr(j, c, T.cores[far], OFF, S.dg_a if c < 4 else S.dg_b), tr(j, c, T.cores[q], ON, near_sem))

    if me == 0:
        def rows(a, b):
            return slice(a * R, b * R)

        def store(j, a, b):
            g.dma_start(T.y[rows(a, b), W * j:W * (j + 1)], T.land[K * j + a:K * j + b]).then_inc(S.stored, 16)

        g.dma_start(T.land[K * q:K * q + 4], T.x[rows(0, 4), :]).then_inc(S.loaded_a, 16)
        g.dma_start(T.land[K * q + 4:K * q + 8], T.x[rows(4, 8), :]).then_inc(S.loaded_b, 16)
        g.wait_ge(S.loaded_a, 16)
        call(to_relay(2, LO), to_relay(0, HI),
             tr(q, 3, core + 4, 0x0F00, S.spread_a), tr(q, 1, core + 4, 0xF000, S.spread_b))
        g.wait_ge(S.loaded_b, 16)
        call(to_relay(4, LO), to_relay(1, HI),
             tr(q, 7, core + 4, 0x0F00, S.spread_b), tr(q, 5, core + 2, 0x3000, S.spread_a),
             tr(q, 6, core + 6, 0xC000, S.spread_a))
        call(to_relay(5, LO), tr(q, 2, T.cores[cb], HI, S.cb_in))
        call(to_relay(6, LO), tr(q, 4, T.cores[cb], HI, S.cb_in))
        call(tr(q, 0, T.cores[sw], LO, S.sw_in), tr(q, 7, T.cores[cb], HI, S.cb_in))
        g.dma_start(T.y[:, W * q:W * (q + 1)], T.x[:, :]).then_inc(S.stored, 16)
        g.wait_ge(S.dg_a, 32)
        store(dg, 0, 4)
        g.wait_ge(S.cb_in, 48)
        store(cb, 0, 8)
        g.wait_ge(S.sw_in, 60)
        store(sw, 0, 8)
        g.wait_ge(S.dg_b, 32)
        store(dg, 4, 8)
        g.wait_ge(S.stored, 80)
    elif me == 2:
        g.wait_ge(S.spread_a, 2)
        call(tr(q, 5, T.cores[cb], OFF, S.cb_in))
        relay(5, 4)
    elif me == 3:
        relay(2, 4)
        relay(3, 4)
    elif me == 4:
        g.wait_ge(S.spread_a, 4)
        call(to_relay(3, LO), tr(q, 3, T.cores[cb], HI, S.cb_in))
        g.wait_ge(S.spread_b, 8)
        call(to_relay(7, OFF))
        call(tr(q, 1, T.cores[sw], OFF, S.sw_in))
    elif me == 5:
        relay(0, 4)
        relay(6, 4)
    elif me == 6:
        g.wait_ge(S.spread_a, 2)
        call(tr(q, 6, T.cores[cb], OFF, S.cb_in))
        relay(4, 4)
    elif me == 7:
        relay(1, 4)
        relay(7, 8)
    if sent[0]:
        g.wait_ge(S.sent, sent[0])
